import numpy as np
import ml_dtypes


def mxq(x, axis, fmt="e4m3"):
    dtype, down = {"e4m3": (ml_dtypes.float8_e4m3fn, 7), "e5m2": (ml_dtypes.float8_e5m2, 14)}[fmt]
    v = np.moveaxis(np.asarray(x, np.float32).astype(ml_dtypes.bfloat16).astype(np.float64), axis, -1)
    blocks = v.reshape(v.shape[:-1] + (-1, 32))
    amax = np.abs(blocks).max(-1, keepdims=True)
    byte = np.maximum(np.where(amax > 0, np.frexp(amax)[1] - 1 + 127, 0) - down, 1)
    scale = np.exp2(byte - 127.0)
    codes = (blocks / scale).astype(np.float32).astype(dtype).astype(np.float64)
    return np.moveaxis((codes * scale).reshape(v.shape), -1, axis)


WIDE = False


def mx_kscale(k):
    if not WIDE:
        return np.ones(k)
    levels = np.array([10, -10, 5, -5, 0])
    if k % 512:
        return np.exp2(np.random.permutation(np.resize(levels, k // 32))).repeat(32)
    a = np.empty((k // 512, 16))
    for p in range(k // 512):
        a[p, :8] = np.random.permutation(np.resize(levels, 8))
        for g in range(8):
            far = levels[np.abs(levels - a[p, g]) >= 10]
            a[p, g + 8] = far[np.random.randint(len(far))]
    return np.exp2(a.ravel()).repeat(32)


def f64(x):
    return np.asarray(x).astype(np.float64)


def striped(idx):
    return np.tile(idx.reshape(-1, 16).T, (8, 1)).astype(np.uint16)


def unstriped(offs):
    return offs[:16].T.reshape(-1).astype(np.int64)


E2M1 = np.array([0.0, 0.5, 1.0, 1.5, 2.0, 3.0, 4.0, 6.0, -0.0, -0.5, -1.0, -1.5, -2.0, -3.0, -4.0, -6.0])


def pack_weight(w, fmt):
    k, n = w.shape
    w = f64(np.asarray(w, np.float32).astype(ml_dtypes.bfloat16)).reshape(k // 32, 32, n)
    amax = np.abs(w).max(1)
    if fmt == "e4m3":
        byte = np.frexp(amax)[1] - 1 + 127 - 7
    else:
        mant, ex = np.frexp(amax / 6.0)
        byte = np.where(mant > 0.5, ex, ex - 1) + 127
    byte = np.clip(np.where(amax > 0, byte, 1), 1, 254)
    scaled = (w * np.exp2(127.0 - byte)[:, None, :]).reshape(k, n).astype(np.float32)
    by_word = np.ascontiguousarray(scaled.reshape(k // 512, 128, 4, n).transpose(0, 1, 3, 2))
    if fmt == "e4m3":
        words = by_word.astype(ml_dtypes.float8_e4m3fn).view(np.uint8)
    else:
        c = by_word.astype(ml_dtypes.float4_e2m1fn).view(np.uint8) & 0xF
        words = (c[..., 0::2] | (c[..., 1::2] << 4)).reshape(k // 512, 128, 2 * n)
    return np.ascontiguousarray(words), np.ascontiguousarray(byte.astype(np.uint8).reshape(k // 512, 16, n))


def unpack_weight(words, scales, fmt):
    g, _, n = scales.shape
    words = np.ascontiguousarray(words).reshape(g, 128, n, -1)
    if fmt == "e4m3":
        vals = words.view(ml_dtypes.float8_e4m3fn).astype(np.float64)
    else:
        nib = np.empty((g, 128, n, 4), np.uint8)
        nib[..., 0::2] = words & 0xF
        nib[..., 1::2] = words >> 4
        vals = E2M1[nib]
    vals = vals * np.repeat(np.exp2(scales.astype(np.float64) - 127.0), 8, axis=1)[..., None]
    return vals.transpose(0, 1, 3, 2).reshape(g * 512, n)


def gelu(v):
    return 0.5 * v * (1.0 + np.tanh(np.sqrt(2.0 / np.pi) * (v + 0.044715 * v**3)))


K, K2, H, N, T, S, P, T2 = 1024, 512, 512, 512, 2048, 1024, 512, 2048


def setup_inputs():
    n = np.random.standard_normal
    s, s2, u = mx_kscale(K)[:, None], mx_kscale(K2)[:, None], mx_kscale(H)[:, None]
    tab_words, tab_scales = pack_weight(n((K, T)) * s, "e4m3")
    tab2_words, tab2_scales = pack_weight(n((K2, T)) * s2, "e4m3")
    w1 = (0.54 * n((K, H)) / s / np.sqrt(K)).astype(np.float32)
    w2_words, w2_scales = pack_weight(n((K2, H)) / s2 * u.T / np.sqrt(K2), "e2m1")
    w3 = (1.5 * n((H, N)) / u / np.sqrt(H)).astype(np.float32)
    wx_words, wx_scales = pack_weight(0.7 * n((K, N)) / s / np.sqrt(K), "e2m1")
    w4 = (n((H, N)) / u / np.sqrt(H)).astype(np.float32)
    gz = (1.5 * np.exp(0.3 * n(H)) * u[:, 0]).astype(np.float32)
    pv = (1.6 * np.exp(0.3 * n(H)) * u[:, 0]).astype(np.float32)
    perm = np.random.permutation(T2)
    return {"tab_words": tab_words, "tab_scales": tab_scales, "tab2_words": tab2_words, "tab2_scales": tab2_scales,
            "offs": striped(np.random.permutation(T)[:S]), "offs2": striped(np.random.permutation(T)[:P]),
            "pos1": striped(np.random.permutation(S)[:P]),
            "offs3": striped(perm[:S]), "offs4": striped(perm[S:S + P]),
            "w1": w1, "w2_words": w2_words, "w2_scales": w2_scales, "w3": w3,
            "wx_words": wx_words, "wx_scales": wx_scales, "w4": w4, "gz": gz, "pv": pv,
            "wg1": np.exp(0.3 * n((128, S))).astype(np.float32), "wg2": np.exp(0.3 * n((128, P))).astype(np.float32),
            "page1": n((N, T2)).astype(np.float32)}


def reference(tab_words, tab_scales, tab2_words, tab2_scales, offs, offs2, pos1, offs3, offs4, w1, w2_words, w2_scales,
              w3, wx_words, wx_scales, w4, gz, pv, wg1, wg2, page1):
    v = unpack_weight(tab_words, tab_scales, "e4m3")[:, unstriped(offs)]
    v2 = unpack_weight(tab2_words, tab2_scales, "e4m3")[:, unstriped(offs2)]
    h1 = mxq(f64(w1), 0, "e4m3").T @ v
    h2 = unpack_weight(w2_words, w2_scales, "e2m1").T @ v2
    z1 = mxq(f64(gz)[:, None] * np.sin(h1), 0, "e4m3")
    z2 = mxq(np.maximum(h2, f64(pv)[:, None] * h1[:, unstriped(pos1)]), 0, "e4m3")
    y1 = mxq(f64(w3), 0, "e4m3").T @ z1 + unpack_weight(wx_words, wx_scales, "e2m1").T @ v
    y2 = mxq(f64(w4), 0, "e4m3").T @ z2
    out = f64(page1).copy()
    out[:, unstriped(offs3)] = np.tile(f64(wg1), (N // 128, 1)) * y1
    out[:, unstriped(offs4)] = np.tile(f64(wg2), (N // 128, 1)) * y2
    return out

@@ -1,0 +1,280 @@
+from contextlib import ExitStack
+
+import concourse.mybir as mybir
+
+K, K2, H, N, T, S, P2, T2 = 1024, 512, 512, 512, 2048, 1024, 512, 2048
+FLOPS = 2 * (K * H * S + K2 * H * P2 + H * N * S + K * N * S + H * N * P2)
+
+F32 = mybir.dt.float32
+BF16 = mybir.dt.bfloat16
+I32 = mybir.dt.int32
+U32 = mybir.dt.uint32
+U16 = mybir.dt.uint16
+U8 = mybir.dt.uint8
+FP8X4 = mybir.dt.float8_e4m3fn_x4
+FP4X4 = mybir.dt.float4_e2m1fn_x4
+MULT = mybir.AluOpType.mult
+MAX = mybir.AluOpType.max
+SIN = mybir.ActivationFunctionType.Sin
+COPY = mybir.ActivationFunctionType.Copy
+
+P = 128
+PACK = 4
+BANK = 512
+TRAIN_CHUNKS = ((0, 256), (256, 512))
+WAGON_CHUNKS = ((0, 256), (256, 512), (512, 1024))
+
+
+def interleave(nc, dst, src):
+    nc.scalar.copy(
+        dst.rearrange("p (c i t) -> p c t i", i=4, t=PACK),
+        src.rearrange("p t (c i) -> p c t i", i=4),
+    )
+
+
+def tile_list_wagon_train_scores_kernel(
+    tc, tab_words, tab_scales, tab2_words, tab2_scales, offs, offs2, pos1, offs3, offs4,
+    w1, w2_words, w2_scales, w3, wx_words, wx_scales, w4, gz, pv, wg1, wg2, page1, out,
+):
+    nc = tc.nc
+    with ExitStack() as ctx:
+        keep = ctx.enter_context(tc.tile_pool(name="keep", bufs=1))
+        ring = ctx.enter_context(tc.tile_pool(name="ring", bufs=3))
+        psum = ctx.enter_context(tc.psum_pool(name="psum", bufs=8))
+
+        def held(shape, dtype, name, slot=None):
+            return keep.tile(shape, dtype, name=name, tag=slot or name, align_bytes=64)
+
+        def load_list(src, name):
+            lst = held(list(src.shape), U16, name)
+            nc.sync.dma_start(lst[:], src)
+            return lst
+
+        def load_words(src, name, slot=None):
+            words = held([P, T], I32, name, slot)
+            nc.sync.dma_start(words[:], src.rearrange("p t i -> p (t i)").bitcast(I32))
+            return words
+
+        def load_rows(src, name, slot=None):
+            rows = held([P, PACK, src.shape[1]], F32, name, slot)
+            nc.sync.dma_start(rows[:], src.rearrange("(p j) c -> p j c", j=PACK))
+            return rows
+
+        def zeroed_plane(width, name):
+            plane = held([P, width], U8, name)
+            nc.vector.memset(plane[:].bitcast(I32), 0)
+            return plane
+
+        def load_plain(src, name, slot):
+            rows = held(list(src.shape), F32, name, slot)
+            nc.sync.dma_start(rows[:], src)
+            return rows
+
+        def block(i):
+            return slice(P * i, P * (i + 1))
+
+        tab_plane = zeroed_plane(T, "tab_plane")
+        w2_plane_raw = zeroed_plane(H, "w2_plane_raw")
+        tab2_plane = zeroed_plane(T, "tab2_plane")
+        wx_plane = zeroed_plane(2 * N, "wx_plane")
+        v1_plane = zeroed_plane(S, "v1_plane")
+        for q in range(4):
+            nc.gpsimd.dma_start(
+                tab_plane[32 * q : 32 * q + 8, :].bitcast(I32), tab_scales[:, 4 * q : 4 * q + 4, :].bitcast(I32)
+            )
+        for q in range(4):
+            nc.gpsimd.dma_start(
+                w2_plane_raw[32 * q : 32 * q + 4, :].bitcast(I32), w2_scales[0, 4 * q : 4 * q + 4, :].bitcast(I32)
+            )
+
+        w2_raw = held([P, H], U16, "w2_raw")
+        nc.sync.dma_start(w2_raw[:].bitcast(I32), w2_words[0].bitcast(I32))
+        idx = load_list(offs, "idx")
+        tab0 = load_words(tab_words[0], "tab0")
+        idx2 = load_list(offs2, "idx2")
+        pilot = load_list(pos1, "pilot")
+        slots2 = load_list(offs4, "slots2")
+        slots1 = load_list(offs3, "slots1")
+        w1_raw0 = load_rows(w1[0:512, :], "w1_raw0")
+        tab1 = load_words(tab_words[1], "tab1")
+        w1_raw1 = [load_rows(w1[512:1024, 256 * u : 256 * (u + 1)], "w1_raw1_%d" % u) for u in range(2)]
+        for q in range(4):
+            nc.sync.dma_start(
+                tab2_plane[32 * q : 32 * q + 4, :].bitcast(I32), tab2_scales[0, 4 * q : 4 * q + 4, :].bitcast(I32)
+            )
+
+        def gather(window, lst, count, dtype, name, slot=None):
+            picked = held([P, count], dtype, name, slot)
+            nc.vector.tensor_copy(picked[:], window.indirect(lst[:]))
+            return picked
+
+        def quantize(src, name):
+            width = src.shape[1] // PACK
+            codes = held([P, width], U32, name + "_codes")
+            plane = held([P, width], U8, name + "_plane")
+            nc.vector.quantize_mx(out=codes[:].bitcast(FP8X4), scales=plane[:], in_=src)
+            return codes, plane
+
+        def deal_w1(dst, raw, m0):
+            count = raw.shape[2] // PACK
+            nc.scalar.copy(
+                dst[:].rearrange("p (t m j) -> p m t j", t=PACK, j=PACK)[:, m0 : m0 + count, :, :],
+                raw[:].rearrange("p j (m t) -> p m t j", t=PACK),
+            )
+
+        w2_codes = held([P, 2 * H], U8, "w2_codes")
+        nc.vector.tensor_copy(
+            w2_codes[:].bitcast(U16).rearrange("p (t m) -> p t m", t=PACK),
+            w2_raw[:].rearrange("p (m t) -> p t m", t=PACK),
+        )
+        gains = held([P, 2, 8], F32, "gains", "w2_raw")
+        pv_col = gains[:, 0, :]
+        gz_col = gains[:, 1, :]
+        nc.gpsimd.dma_start(pv_col[:, 0:PACK], pv.rearrange("(p t) -> p t", t=PACK))
+        nc.gpsimd.dma_start(gz_col[:, 0:PACK], gz.rearrange("(p t) -> p t", t=PACK))
+        for q in range(4):
+            nc.gpsimd.dma_start(
+                wx_plane[32 * q : 32 * q + 4, :].bitcast(I32).rearrange("r (a c) -> r a c", a=2),
+                wx_scales[:, 4 * q : 4 * q + 4, :].bitcast(I32).rearrange("a r c -> r a c"),
+            )
+
+        pages = {}
+        v0 = gather(tab0[:].bitcast(U32), idx, S, U32, "v0")
+        tab2 = load_words(tab2_words[0], "tab2", "tab0")
+        v_plane = gather(tab_plane[:], idx, S, U8, "v_plane")
+        nc.gpsimd.dma_start(v1_plane[0:100, :].bitcast(I32), v_plane[4:104, :].bitcast(I32))
+        w1_bf0 = held([P, PACK * H], BF16, "w1_bf0")
+        deal_w1(w1_bf0, w1_raw0, 0)
+        w4_raw = load_rows(w4, "w4_raw", "w1_raw0")
+        v1 = gather(tab1[:].bitcast(U32), idx, S, U32, "v1", "tab_plane")
+        pages[0] = load_plain(page1[block(0), :], "page0", "tab1")
+        w1_q0 = quantize(w1_bf0[:], "w1_0")
+        v2_plane = gather(tab2_plane[:], idx2, P2, U8, "v2_plane", "w1_bf0")
+        w2_plane = held([P, H], U8, "w2_plane")
+        nc.vector.tensor_copy(
+            w2_plane[:].rearrange("p (t m) -> p t m", t=PACK),
+            w2_plane_raw[:].rearrange("p (m t) -> p t m", t=PACK),
+        )
+        w1_bf1 = held([P, PACK * H], BF16, "w1_bf1")
+        for u in range(2):
+            deal_w1(w1_bf1, w1_raw1[u], 64 * u)
+        wg2_sb = load_plain(wg2, "wg2_sb", "w1_raw1_0")
+        pages[1] = load_plain(page1[block(1), :], "page1", "w1_raw1_1")
+        w1_q1 = quantize(w1_bf1[:], "w1_1")
+        pages[2] = load_plain(page1[block(2), :], "page2", "w1_bf1")
+        v2 = gather(tab2[:].bitcast(U32), idx2, P2, U32, "v2")
+        pages[3] = load_plain(page1[block(3), :], "page3", "tab0")
+
+        def mx(acc, lhs, lhs_plane, rhs, rhs_plane, start, stop):
+            nc.tensor.matmul_mx(
+                out=acc, lhsT=lhs, lhsT_scale=lhs_plane, rhs=rhs, rhs_scale=rhs_plane, start=start, stop=stop
+            )
+
+        h1_acc = {}
+        for t in range(PACK):
+            for u in range(2):
+                cols = slice(BANK * u, BANK * (u + 1))
+                h1_acc[t, u] = psum.tile([P, BANK], F32, name="acc")
+                mx(h1_acc[t, u][:], w1_q0[0][:, block(t)].bitcast(FP8X4), w1_q0[1][:, block(t)],
+                   v0[:, cols].bitcast(FP8X4), v_plane[:, cols], True, False)
+        h1 = []
+        h2_acc = []
+        for t in range(PACK):
+            h1.append(held([P, S], F32, "h1_%d" % t))
+            for u in range(2):
+                cols = slice(BANK * u, BANK * (u + 1))
+                mx(h1_acc[t, u][:], w1_q1[0][:, block(t)].bitcast(FP8X4), w1_q1[1][:, block(t)],
+                   v1[:, cols].bitcast(FP8X4), v_plane[4:P, cols], False, True)
+                nc.scalar.copy(h1[t][:, cols], h1_acc[t, u][:])
+            h2_acc.append(psum.tile([P, BANK], F32, name="acc"))
+            mx(h2_acc[t][:], w2_codes[:, 2 * P * t : 2 * P * (t + 1)].bitcast(FP4X4), w2_plane[:, block(t)],
+               v2[:].bitcast(FP8X4), v2_plane[:], True, True)
+
+        def quantize_weight_half(raw, u, name, slot):
+            bf = held([P, PACK * 256], BF16, name + "_bf", slot)
+            interleave(nc, bf[:], raw[:, :, 256 * u : 256 * (u + 1)])
+            return quantize(bf[:], name)
+
+        def z2_rows(c0, c1):
+            rows = held([P, PACK, c1 - c0], BF16, "z2_rows%d" % c0)
+            for t in range(PACK):
+                picked = held([P, c1 - c0], F32, "picked%d_%d" % (c0, t))
+                nc.vector.tensor_copy(picked[:], h1[t][:].indirect(pilot[:, c0 // 16 : c1 // 16]))
+                nc.vector.scalar_tensor_tensor(
+                    rows[:, t, :], picked[:], pv_col[:, t : t + 1], h2_acc[t][:, c0:c1], MULT, MAX
+                )
+            return rows
+
+        def z1_rows(c0, c1):
+            rows = held([P, PACK, c1 - c0], BF16, "z1_rows%d" % c0)
+            sine = held([P, PACK, c1 - c0], F32, "sine%d" % c0, "z2_rows0")
+            for t in range(PACK):
+                nc.scalar.activation(sine[:, t, :], h1[t][:, c0:c1], SIN)
+            for t in range(PACK):
+                nc.scalar.activation(rows[:, t, :], sine[:, t, :], COPY, scale=gz_col[:, t : t + 1])
+            return rows
+
+        def quantize_rows(rows, name):
+            bf = held([P, PACK * rows.shape[2]], BF16, name + "_bf")
+            interleave(nc, bf[:], rows[:])
+            return quantize(bf[:], name)
+
+        def scatter(n, lst, c0, c1, y, gains):
+            nc.vector.tensor_tensor(pages[n][:].indirect(lst[:, c0 // 16 : c1 // 16]), y, gains[:, c0:c1], MULT)
+
+        def train_scores(u, z2_q, w4_q, c0, c1):
+            width = c1 - c0
+            acc = psum.tile([P, BANK], F32, name="acc")
+            for e in range(2):
+                mx(acc[:, width * e : width * (e + 1)], w4_q[0][:, block(e)].bitcast(FP8X4), w4_q[1][:, block(e)],
+                   z2_q[0][:].bitcast(FP8X4), z2_q[1][:], True, True)
+            y = ring.tile([P, BANK], F32, name="y", bufs=6)
+            nc.scalar.copy(y[:], acc[:])
+            for e in range(2):
+                scatter(2 * u + e, slots2, c0, c1, y[:, width * e : width * (e + 1)], wg2_sb)
+
+        def wagon_scores(ns, z1_q, w3_q, c0, c1):
+            width = c1 - c0
+            acc = psum.tile([P, BANK], F32, name="acc")
+            for e, n in enumerate(ns):
+                dst = acc[:, width * e : width * (e + 1)]
+                for a, (words, plane) in enumerate(((v0, v_plane), (v1, v1_plane))):
+                    mx(dst, wx_codes[:, a, 2 * P * n : 2 * P * (n + 1)].bitcast(FP4X4),
+                       wx_plane[:, N * a + P * n : N * a + P * (n + 1)],
+                       words[:, c0:c1].bitcast(FP8X4), plane[:, c0:c1], a == 0, False)
+                w3_codes, w3_plane = w3_q[n // 2]
+                mx(dst, w3_codes[:, block(n % 2)].bitcast(FP8X4), w3_plane[:, block(n % 2)],
+                   z1_q[0][:].bitcast(FP8X4), z1_q[1][:], False, True)
+            y = ring.tile([P, BANK], F32, name="y", bufs=6)
+            nc.scalar.copy(y[:], acc[:])
+            for e, n in enumerate(ns):
+                scatter(n, slots1, c0, c1, y[:, width * e : width * (e + 1)], wg1_sb)
+                if c1 == S:
+                    nc.sync.dma_start(out[block(n), :], pages[n][:])
+
+        (a0, a1), (b0, b1) = TRAIN_CHUNKS
+        rows_a = z2_rows(a0, a1)
+        w3_raw = load_rows(w3, "w3_raw", "picked0_2")
+        wx_codes = held([P, 2, 2 * N], U8, "wx_codes", "picked0_3")
+        nc.sync.dma_start(wx_codes[:].bitcast(I32), wx_words.bitcast(I32).rearrange("a p c -> p a c"))
+        w4_q = [quantize_weight_half(w4_raw, 0, "w4_0", "picked0_0")]
+        z2_a = quantize_rows(rows_a, "z2_a")
+        rows_b = z2_rows(b0, b1)
+        wg1_sb = load_plain(wg1, "wg1_sb", "picked256_0")
+        train_scores(0, z2_a, w4_q[0], a0, a1)
+        w4_q.append(quantize_weight_half(w4_raw, 1, "w4_1", "picked0_1"))
+        train_scores(1, z2_a, w4_q[1], a0, a1)
+        z2_b = quantize_rows(rows_b, "z2_b")
+        train_scores(0, z2_b, w4_q[0], b0, b1)
+        z1_q = quantize_rows(z1_rows(*WAGON_CHUNKS[0]), "z1_0")
+        w3_q = [quantize_weight_half(w3_raw, u, "w3_%d" % u, slot) for u, slot in enumerate(("z2_rows256", "z2_b_bf"))]
+        train_scores(1, z2_b, w4_q[1], b0, b1)
+        for i, (c0, c1) in enumerate(WAGON_CHUNKS):
+            per_bank = BANK // (c1 - c0)
+            groups = [range(n0, n0 + per_bank) for n0 in range(0, 4, per_bank)]
+            for ns in groups[:-1]:
+                wagon_scores(ns, z1_q, w3_q, c0, c1)
+            if i + 1 < len(WAGON_CHUNKS):
+                z1_next = quantize_rows(z1_rows(*WAGON_CHUNKS[i + 1]), "z1_%d" % (i + 1))
+            wagon_scores(groups[-1], z1_q, w3_q, c0, c1)
+            z1_q = z1_next

@@ -39,7 +39,6 @@ def tile_list_wagon_train_scores_kernel(
     nc = tc.nc
     with ExitStack() as ctx:
         keep = ctx.enter_context(tc.tile_pool(name="keep", bufs=1))
-        ring = ctx.enter_context(tc.tile_pool(name="ring", bufs=3))
         psum = ctx.enter_context(tc.psum_pool(name="psum", bufs=8))
 
         def held(shape, dtype, name, slot=None):
@@ -60,9 +59,9 @@ def tile_list_wagon_train_scores_kernel(
             nc.sync.dma_start(rows[:], src.rearrange("(p j) c -> p j c", j=PACK))
             return rows
 
-        def zeroed_plane(width, name):
+        def zeroed_plane(engine, width, name):
             plane = held([P, width], U8, name)
-            nc.vector.memset(plane[:].bitcast(I32), 0)
+            engine.memset(plane[:].bitcast(I32), 0)
             return plane
 
         def load_plain(src, name, slot):
@@ -73,22 +72,26 @@ def tile_list_wagon_train_scores_kernel(
         def block(i):
             return slice(P * i, P * (i + 1))
 
-        tab_plane = zeroed_plane(T, "tab_plane")
-        w2_plane_raw = zeroed_plane(H, "w2_plane_raw")
-        tab2_plane = zeroed_plane(T, "tab2_plane")
-        wx_plane = zeroed_plane(2 * N, "wx_plane")
-        v1_plane = zeroed_plane(S, "v1_plane")
+        def load_scales(queue, plane, src):
+            for q in range(4):
+                queue.dma_start(plane[32 * q : 32 * q + 4, :].bitcast(I32), src[4 * q : 4 * q + 4, :].bitcast(I32))
+
+        tab_plane = zeroed_plane(nc.gpsimd, T, "tab_plane")
+        w2_plane_raw = zeroed_plane(nc.vector, H, "w2_plane_raw")
+        tab2_plane = zeroed_plane(nc.vector, T, "tab2_plane")
+        wx_plane = zeroed_plane(nc.vector, 2 * N, "wx_plane")
+        v1_plane = zeroed_plane(nc.vector, S, "v1_plane")
         for q in range(4):
             nc.gpsimd.dma_start(
                 tab_plane[32 * q : 32 * q + 8, :].bitcast(I32), tab_scales[:, 4 * q : 4 * q + 4, :].bitcast(I32)
             )
+        load_scales(nc.gpsimd, w2_plane_raw, w2_scales[0])
         for q in range(4):
             nc.gpsimd.dma_start(
-                w2_plane_raw[32 * q : 32 * q + 4, :].bitcast(I32), w2_scales[0, 4 * q : 4 * q + 4, :].bitcast(I32)
+                wx_plane[32 * q : 32 * q + 4, :].bitcast(I32).rearrange("r (a c) -> r a c", a=2),
+                wx_scales[:, 4 * q : 4 * q + 4, :].bitcast(I32).rearrange("a r c -> r a c"),
             )
 
-        w2_raw = held([P, H], U16, "w2_raw")
-        nc.sync.dma_start(w2_raw[:].bitcast(I32), w2_words[0].bitcast(I32))
         idx = load_list(offs, "idx")
         tab0 = load_words(tab_words[0], "tab0")
         idx2 = load_list(offs2, "idx2")
@@ -98,19 +101,18 @@ def tile_list_wagon_train_scores_kernel(
         w1_raw0 = load_rows(w1[0:512, :], "w1_raw0")
         tab1 = load_words(tab_words[1], "tab1")
         w1_raw1 = [load_rows(w1[512:1024, 256 * u : 256 * (u + 1)], "w1_raw1_%d" % u) for u in range(2)]
-        for q in range(4):
-            nc.sync.dma_start(
-                tab2_plane[32 * q : 32 * q + 4, :].bitcast(I32), tab2_scales[0, 4 * q : 4 * q + 4, :].bitcast(I32)
-            )
+        w2_raw = held([P, H], U16, "w2_raw")
+        nc.sync.dma_start(w2_raw[:].bitcast(I32), w2_words[0].bitcast(I32))
+        load_scales(nc.sync, tab2_plane, tab2_scales[0])
 
         def gather(window, lst, count, dtype, name, slot=None):
             picked = held([P, count], dtype, name, slot)
             nc.vector.tensor_copy(picked[:], window.indirect(lst[:]))
             return picked
 
-        def quantize(src, name):
+        def quantize(src, name, slot=None):
             width = src.shape[1] // PACK
-            codes = held([P, width], U32, name + "_codes")
+            codes = held([P, width], U32, name + "_codes", slot)
             plane = held([P, width], U8, name + "_plane")
             nc.vector.quantize_mx(out=codes[:].bitcast(FP8X4), scales=plane[:], in_=src)
             return codes, plane
@@ -122,48 +124,40 @@ def tile_list_wagon_train_scores_kernel(
                 raw[:].rearrange("p j (m t) -> p m t j", t=PACK),
             )
 
-        w2_codes = held([P, 2 * H], U8, "w2_codes")
-        nc.vector.tensor_copy(
-            w2_codes[:].bitcast(U16).rearrange("p (t m) -> p t m", t=PACK),
-            w2_raw[:].rearrange("p (m t) -> p t m", t=PACK),
-        )
-        gains = held([P, 2, 8], F32, "gains", "w2_raw")
-        pv_col = gains[:, 0, :]
-        gz_col = gains[:, 1, :]
-        nc.gpsimd.dma_start(pv_col[:, 0:PACK], pv.rearrange("(p t) -> p t", t=PACK))
-        nc.gpsimd.dma_start(gz_col[:, 0:PACK], gz.rearrange("(p t) -> p t", t=PACK))
-        for q in range(4):
-            nc.gpsimd.dma_start(
-                wx_plane[32 * q : 32 * q + 4, :].bitcast(I32).rearrange("r (a c) -> r a c", a=2),
-                wx_scales[:, 4 * q : 4 * q + 4, :].bitcast(I32).rearrange("a r c -> r a c"),
-            )
-
         pages = {}
         v0 = gather(tab0[:].bitcast(U32), idx, S, U32, "v0")
         tab2 = load_words(tab2_words[0], "tab2", "tab0")
         v_plane = gather(tab_plane[:], idx, S, U8, "v_plane")
+        gains = held([P, 2, 8], F32, "gains", "tab_plane")
+        pv_col = gains[:, 0, :]
+        gz_col = gains[:, 1, :]
+        nc.gpsimd.dma_start(pv_col[:, 0:PACK], pv.rearrange("(p t) -> p t", t=PACK))
+        nc.gpsimd.dma_start(gz_col[:, 0:PACK], gz.rearrange("(p t) -> p t", t=PACK))
         nc.gpsimd.dma_start(v1_plane[0:100, :].bitcast(I32), v_plane[4:104, :].bitcast(I32))
         w1_bf0 = held([P, PACK * H], BF16, "w1_bf0")
         deal_w1(w1_bf0, w1_raw0, 0)
-        w4_raw = load_rows(w4, "w4_raw", "w1_raw0")
-        v1 = gather(tab1[:].bitcast(U32), idx, S, U32, "v1", "tab_plane")
-        pages[0] = load_plain(page1[block(0), :], "page0", "tab1")
+        v1 = gather(tab1[:].bitcast(U32), idx, S, U32, "v1")
+        w4_raw = load_rows(w4, "w4_raw", "tab1")
         w1_q0 = quantize(w1_bf0[:], "w1_0")
         v2_plane = gather(tab2_plane[:], idx2, P2, U8, "v2_plane", "w1_bf0")
-        w2_plane = held([P, H], U8, "w2_plane")
+        wg2_sb = load_plain(wg2, "wg2_sb", "tab2_plane")
+        w1_bf1 = held([P, PACK * H], BF16, "w1_bf1")
+        for u in range(2):
+            deal_w1(w1_bf1, w1_raw1[u], 64 * u)
+        pages[1] = load_plain(page1[block(1), :], "page1", "w1_raw1_0")
+        w3_raw = load_rows(w3, "w3_raw", "w1_raw1_1")
+        w1_q1 = quantize(w1_bf1[:], "w1_1")
+        w2_plane = held([P, H], U8, "w2_plane", "w1_bf1")
         nc.vector.tensor_copy(
             w2_plane[:].rearrange("p (t m) -> p t m", t=PACK),
             w2_plane_raw[:].rearrange("p (m t) -> p t m", t=PACK),
         )
-        w1_bf1 = held([P, PACK * H], BF16, "w1_bf1")
-        for u in range(2):
-            deal_w1(w1_bf1, w1_raw1[u], 64 * u)
-        wg2_sb = load_plain(wg2, "wg2_sb", "w1_raw1_0")
-        pages[1] = load_plain(page1[block(1), :], "page1", "w1_raw1_1")
-        w1_q1 = quantize(w1_bf1[:], "w1_1")
-        pages[2] = load_plain(page1[block(2), :], "page2", "w1_bf1")
-        v2 = gather(tab2[:].bitcast(U32), idx2, P2, U32, "v2")
-        pages[3] = load_plain(page1[block(3), :], "page3", "tab0")
+        w2_codes = held([P, 2 * H], U8, "w2_codes", "w2_plane_raw")
+        nc.vector.tensor_copy(
+            w2_codes[:].bitcast(U16).rearrange("p (t m) -> p t m", t=PACK),
+            w2_raw[:].rearrange("p (m t) -> p t m", t=PACK),
+        )
+        v2 = gather(tab2[:].bitcast(U32), idx2, P2, U32, "v2", "w2_raw")
 
         def mx(acc, lhs, lhs_plane, rhs, rhs_plane, start, stop):
             nc.tensor.matmul_mx(
@@ -177,6 +171,7 @@ def tile_list_wagon_train_scores_kernel(
                 h1_acc[t, u] = psum.tile([P, BANK], F32, name="acc")
                 mx(h1_acc[t, u][:], w1_q0[0][:, block(t)].bitcast(FP8X4), w1_q0[1][:, block(t)],
                    v0[:, cols].bitcast(FP8X4), v_plane[:, cols], True, False)
+        pages[0] = load_plain(page1[block(0), :], "page0", "w1_0_codes")
         h1 = []
         h2_acc = []
         for t in range(PACK):
@@ -190,6 +185,10 @@ def tile_list_wagon_train_scores_kernel(
             mx(h2_acc[t][:], w2_codes[:, 2 * P * t : 2 * P * (t + 1)].bitcast(FP4X4), w2_plane[:, block(t)],
                v2[:].bitcast(FP8X4), v2_plane[:], True, True)
 
+        pages[2] = load_plain(page1[block(2), :], "page2", "w1_bf0")
+        pages[3] = load_plain(page1[block(3), :], "page3", "w2_raw")
+        picked_slots = ("tab0", "picked1", "picked2", "picked3")
+
         def quantize_weight_half(raw, u, name, slot):
             bf = held([P, PACK * 256], BF16, name + "_bf", slot)
             interleave(nc, bf[:], raw[:, :, 256 * u : 256 * (u + 1)])
@@ -198,7 +197,7 @@ def tile_list_wagon_train_scores_kernel(
         def z2_rows(c0, c1):
             rows = held([P, PACK, c1 - c0], BF16, "z2_rows%d" % c0)
             for t in range(PACK):
-                picked = held([P, c1 - c0], F32, "picked%d_%d" % (c0, t))
+                picked = held([P, c1 - c0], F32, "picked%d_%d" % (c0, t), picked_slots[t])
                 nc.vector.tensor_copy(picked[:], h1[t][:].indirect(pilot[:, c0 // 16 : c1 // 16]))
                 nc.vector.scalar_tensor_tensor(
                     rows[:, t, :], picked[:], pv_col[:, t : t + 1], h2_acc[t][:, c0:c1], MULT, MAX
@@ -207,17 +206,17 @@ def tile_list_wagon_train_scores_kernel(
 
         def z1_rows(c0, c1):
             rows = held([P, PACK, c1 - c0], BF16, "z1_rows%d" % c0)
-            sine = held([P, PACK, c1 - c0], F32, "sine%d" % c0, "z2_rows0")
+            sine = held([P, PACK, c1 - c0], F32, "sine%d" % c0, "tab1")
             for t in range(PACK):
                 nc.scalar.activation(sine[:, t, :], h1[t][:, c0:c1], SIN)
             for t in range(PACK):
                 nc.scalar.activation(rows[:, t, :], sine[:, t, :], COPY, scale=gz_col[:, t : t + 1])
             return rows
 
-        def quantize_rows(rows, name):
+        def quantize_rows(rows, name, slot=None):
             bf = held([P, PACK * rows.shape[2]], BF16, name + "_bf")
             interleave(nc, bf[:], rows[:])
-            return quantize(bf[:], name)
+            return quantize(bf[:], name, slot)
 
         def scatter(n, lst, c0, c1, y, gains):
             nc.vector.tensor_tensor(pages[n][:].indirect(lst[:, c0 // 16 : c1 // 16]), y, gains[:, c0:c1], MULT)
@@ -228,7 +227,7 @@ def tile_list_wagon_train_scores_kernel(
             for e in range(2):
                 mx(acc[:, width * e : width * (e + 1)], w4_q[0][:, block(e)].bitcast(FP8X4), w4_q[1][:, block(e)],
                    z2_q[0][:].bitcast(FP8X4), z2_q[1][:], True, True)
-            y = ring.tile([P, BANK], F32, name="y", bufs=6)
+            y = held([P, BANK], F32, "y2_%d_%d" % (c0, u))
             nc.scalar.copy(y[:], acc[:])
             for e in range(2):
                 scatter(2 * u + e, slots2, c0, c1, y[:, width * e : width * (e + 1)], wg2_sb)
@@ -245,7 +244,7 @@ def tile_list_wagon_train_scores_kernel(
                 w3_codes, w3_plane = w3_q[n // 2]
                 mx(dst, w3_codes[:, block(n % 2)].bitcast(FP8X4), w3_plane[:, block(n % 2)],
                    z1_q[0][:].bitcast(FP8X4), z1_q[1][:], False, True)
-            y = ring.tile([P, BANK], F32, name="y", bufs=6)
+            y = held([P, BANK], F32, "y1_%d_%d" % (c0, ns[0]))
             nc.scalar.copy(y[:], acc[:])
             for e, n in enumerate(ns):
                 scatter(n, slots1, c0, c1, y[:, width * e : width * (e + 1)], wg1_sb)
@@ -254,19 +253,18 @@ def tile_list_wagon_train_scores_kernel(
 
         (a0, a1), (b0, b1) = TRAIN_CHUNKS
         rows_a = z2_rows(a0, a1)
-        w3_raw = load_rows(w3, "w3_raw", "picked0_2")
-        wx_codes = held([P, 2, 2 * N], U8, "wx_codes", "picked0_3")
-        nc.sync.dma_start(wx_codes[:].bitcast(I32), wx_words.bitcast(I32).rearrange("a p c -> p a c"))
-        w4_q = [quantize_weight_half(w4_raw, 0, "w4_0", "picked0_0")]
+        w4_q = [quantize_weight_half(w4_raw, 0, "w4_0", "w1_1_codes")]
         z2_a = quantize_rows(rows_a, "z2_a")
         rows_b = z2_rows(b0, b1)
-        wg1_sb = load_plain(wg1, "wg1_sb", "picked256_0")
+        wx_codes = held([P, 2, 2 * N], U8, "wx_codes", picked_slots[0])
+        nc.sync.dma_start(wx_codes[:].bitcast(I32), wx_words.bitcast(I32).rearrange("a p c -> p a c"))
+        wg1_sb = load_plain(wg1, "wg1_sb", picked_slots[1])
         train_scores(0, z2_a, w4_q[0], a0, a1)
-        w4_q.append(quantize_weight_half(w4_raw, 1, "w4_1", "picked0_1"))
+        w4_q.append(quantize_weight_half(w4_raw, 1, "w4_1", "w1_1_plane"))
         train_scores(1, z2_a, w4_q[1], a0, a1)
         z2_b = quantize_rows(rows_b, "z2_b")
         train_scores(0, z2_b, w4_q[0], b0, b1)
-        z1_q = quantize_rows(z1_rows(*WAGON_CHUNKS[0]), "z1_0")
+        z1_q = quantize_rows(z1_rows(*WAGON_CHUNKS[0]), "z1_0", "y2_0_1")
         w3_q = [quantize_weight_half(w3_raw, u, "w3_%d" % u, slot) for u, slot in enumerate(("z2_rows256", "z2_b_bf"))]
         train_scores(1, z2_b, w4_q[1], b0, b1)
         for i, (c0, c1) in enumerate(WAGON_CHUNKS):
@@ -275,6 +273,6 @@ def tile_list_wagon_train_scores_kernel(
             for ns in groups[:-1]:
                 wagon_scores(ns, z1_q, w3_q, c0, c1)
             if i + 1 < len(WAGON_CHUNKS):
-                z1_next = quantize_rows(z1_rows(*WAGON_CHUNKS[i + 1]), "z1_%d" % (i + 1))
+                z1_next = quantize_rows(z1_rows(*WAGON_CHUNKS[i + 1]), "z1_%d" % (i + 1), "y1_%d_0" % c0)
             wagon_scores(groups[-1], z1_q, w3_q, c0, c1)
             z1_q = z1_next

@@ -59,8 +59,8 @@ def tile_list_wagon_train_scores_kernel(
             nc.sync.dma_start(rows[:], src.rearrange("(p j) c -> p j c", j=PACK))
             return rows
 
-        def zeroed_plane(engine, width, name):
-            plane = held([P, width], U8, name)
+        def zeroed_plane(engine, width, name, slot=None):
+            plane = held([P, width], U8, name, slot)
             engine.memset(plane[:].bitcast(I32), 0)
             return plane
 
@@ -76,34 +76,40 @@ def tile_list_wagon_train_scores_kernel(
             for q in range(4):
                 queue.dma_start(plane[32 * q : 32 * q + 4, :].bitcast(I32), src[4 * q : 4 * q + 4, :].bitcast(I32))
 
-        tab_plane = zeroed_plane(nc.gpsimd, T, "tab_plane")
+        tab_plane = zeroed_plane(nc.vector, T, "tab_plane")
+        tab2_plane = zeroed_plane(nc.gpsimd, T, "tab2_plane")
         w2_plane_raw = zeroed_plane(nc.vector, H, "w2_plane_raw")
-        tab2_plane = zeroed_plane(nc.vector, T, "tab2_plane")
-        wx_plane = zeroed_plane(nc.vector, 2 * N, "wx_plane")
         v1_plane = zeroed_plane(nc.vector, S, "v1_plane")
-        for q in range(4):
-            nc.gpsimd.dma_start(
-                tab_plane[32 * q : 32 * q + 8, :].bitcast(I32), tab_scales[:, 4 * q : 4 * q + 4, :].bitcast(I32)
-            )
+        load_scales(nc.gpsimd, tab2_plane, tab2_scales[0])
         load_scales(nc.gpsimd, w2_plane_raw, w2_scales[0])
-        for q in range(4):
-            nc.gpsimd.dma_start(
-                wx_plane[32 * q : 32 * q + 4, :].bitcast(I32).rearrange("r (a c) -> r a c", a=2),
-                wx_scales[:, 4 * q : 4 * q + 4, :].bitcast(I32).rearrange("a r c -> r a c"),
-            )
 
         idx = load_list(offs, "idx")
-        tab0 = load_words(tab_words[0], "tab0")
         idx2 = load_list(offs2, "idx2")
         pilot = load_list(pos1, "pilot")
         slots2 = load_list(offs4, "slots2")
         slots1 = load_list(offs3, "slots1")
-        w1_raw0 = load_rows(w1[0:512, :], "w1_raw0")
-        tab1 = load_words(tab_words[1], "tab1")
-        w1_raw1 = [load_rows(w1[512:1024, 256 * u : 256 * (u + 1)], "w1_raw1_%d" % u) for u in range(2)]
-        w2_raw = held([P, H], U16, "w2_raw")
-        nc.sync.dma_start(w2_raw[:].bitcast(I32), w2_words[0].bitcast(I32))
-        load_scales(nc.sync, tab2_plane, tab2_scales[0])
+        w2_raw = []
+        for u in range(2):
+            w2_raw.append(held([P, H // 2], U16, "w2_raw%d" % u))
+            nc.sync.dma_start(w2_raw[u][:].bitcast(I32), w2_words[0, :, 512 * u : 512 * (u + 1)].bitcast(I32))
+        tab0 = load_words(tab_words[0], "tab0")
+        for q in range(4):
+            nc.sync.dma_start(
+                tab_plane[32 * q : 32 * q + 8, :].bitcast(I32), tab_scales[:, 4 * q : 4 * q + 4, :].bitcast(I32)
+            )
+        w2_codes = held([P, 2 * H], U8, "w2_codes")
+        for u in range(2):
+            nc.vector.tensor_copy(
+                w2_codes[:].bitcast(U16).rearrange("p (t m) -> p t m", t=PACK)[:, :, 64 * u : 64 * (u + 1)],
+                w2_raw[u][:].rearrange("p (m t) -> p t m", t=PACK),
+            )
+        w1_all = held([P, 2 * PACK * H], F32, "w1_all", "w2_raw0")
+        w1_raw0 = w1_all[:, 0:2048].rearrange("p (j c) -> p j c", j=PACK)
+        w1_raw1 = [w1_all[:, 2048 + 1024 * u : 3072 + 1024 * u].rearrange("p (j c) -> p j c", j=PACK) for u in range(2)]
+        nc.sync.dma_start(w1_raw0, w1[0:512, :].rearrange("(p j) c -> p j c", j=PACK))
+        tab1 = load_words(tab_words[1], "tab1", "w2_raw1")
+        for u in range(2):
+            nc.sync.dma_start(w1_raw1[u], w1[512:1024, 256 * u : 256 * (u + 1)].rearrange("(p j) c -> p j c", j=PACK))
 
         def gather(window, lst, count, dtype, name, slot=None):
             picked = held([P, count], dtype, name, slot)
@@ -121,7 +127,7 @@ def tile_list_wagon_train_scores_kernel(
             count = raw.shape[2] // PACK
             nc.scalar.copy(
                 dst[:].rearrange("p (t m j) -> p m t j", t=PACK, j=PACK)[:, m0 : m0 + count, :, :],
-                raw[:].rearrange("p j (m t) -> p m t j", t=PACK),
+                raw.rearrange("p j (m t) -> p m t j", t=PACK),
             )
 
         pages = {}
@@ -131,33 +137,27 @@ def tile_list_wagon_train_scores_kernel(
         gains = held([P, 2, 8], F32, "gains", "tab_plane")
         pv_col = gains[:, 0, :]
         gz_col = gains[:, 1, :]
-        nc.gpsimd.dma_start(pv_col[:, 0:PACK], pv.rearrange("(p t) -> p t", t=PACK))
-        nc.gpsimd.dma_start(gz_col[:, 0:PACK], gz.rearrange("(p t) -> p t", t=PACK))
-        nc.gpsimd.dma_start(v1_plane[0:100, :].bitcast(I32), v_plane[4:104, :].bitcast(I32))
+        nc.sync.dma_start(pv_col[:, 0:PACK], pv.rearrange("(p t) -> p t", t=PACK))
+        nc.sync.dma_start(gz_col[:, 0:PACK], gz.rearrange("(p t) -> p t", t=PACK))
+        nc.sync.dma_start(v1_plane[0:100, :].bitcast(I32), v_plane[4:104, :].bitcast(I32))
         w1_bf0 = held([P, PACK * H], BF16, "w1_bf0")
         deal_w1(w1_bf0, w1_raw0, 0)
         v1 = gather(tab1[:].bitcast(U32), idx, S, U32, "v1")
-        w4_raw = load_rows(w4, "w4_raw", "tab1")
+        w4_raw = load_rows(w4, "w4_raw", "w2_raw1")
         w1_q0 = quantize(w1_bf0[:], "w1_0")
         v2_plane = gather(tab2_plane[:], idx2, P2, U8, "v2_plane", "w1_bf0")
         wg2_sb = load_plain(wg2, "wg2_sb", "tab2_plane")
         w1_bf1 = held([P, PACK * H], BF16, "w1_bf1")
         for u in range(2):
             deal_w1(w1_bf1, w1_raw1[u], 64 * u)
-        pages[1] = load_plain(page1[block(1), :], "page1", "w1_raw1_0")
-        w3_raw = load_rows(w3, "w3_raw", "w1_raw1_1")
+        pages[1] = load_plain(page1[block(1), :], "page1", "w2_raw0")
         w1_q1 = quantize(w1_bf1[:], "w1_1")
         w2_plane = held([P, H], U8, "w2_plane", "w1_bf1")
         nc.vector.tensor_copy(
             w2_plane[:].rearrange("p (t m) -> p t m", t=PACK),
             w2_plane_raw[:].rearrange("p (m t) -> p t m", t=PACK),
         )
-        w2_codes = held([P, 2 * H], U8, "w2_codes", "w2_plane_raw")
-        nc.vector.tensor_copy(
-            w2_codes[:].bitcast(U16).rearrange("p (t m) -> p t m", t=PACK),
-            w2_raw[:].rearrange("p (m t) -> p t m", t=PACK),
-        )
-        v2 = gather(tab2[:].bitcast(U32), idx2, P2, U32, "v2", "w2_raw")
+        v2 = gather(tab2[:].bitcast(U32), idx2, P2, U32, "v2", "w2_plane_raw")
 
         def mx(acc, lhs, lhs_plane, rhs, rhs_plane, start, stop):
             nc.tensor.matmul_mx(
@@ -172,6 +172,7 @@ def tile_list_wagon_train_scores_kernel(
                 mx(h1_acc[t, u][:], w1_q0[0][:, block(t)].bitcast(FP8X4), w1_q0[1][:, block(t)],
                    v0[:, cols].bitcast(FP8X4), v_plane[:, cols], True, False)
         pages[0] = load_plain(page1[block(0), :], "page0", "w1_0_codes")
+        w3_raw = load_rows(w3, "w3_raw", "w1_0_plane")
         h1 = []
         h2_acc = []
         for t in range(PACK):
@@ -186,7 +187,7 @@ def tile_list_wagon_train_scores_kernel(
                v2[:].bitcast(FP8X4), v2_plane[:], True, True)
 
         pages[2] = load_plain(page1[block(2), :], "page2", "w1_bf0")
-        pages[3] = load_plain(page1[block(3), :], "page3", "w2_raw")
+        pages[3] = load_plain(page1[block(3), :], "page3", "w2_plane_raw")
         picked_slots = ("tab0", "picked1", "picked2", "picked3")
 
         def quantize_weight_half(raw, u, name, slot):
@@ -206,7 +207,7 @@ def tile_list_wagon_train_scores_kernel(
 
         def z1_rows(c0, c1):
             rows = held([P, PACK, c1 - c0], BF16, "z1_rows%d" % c0)
-            sine = held([P, PACK, c1 - c0], F32, "sine%d" % c0, "tab1")
+            sine = held([P, PACK, c1 - c0], F32, "sine%d" % c0, "w2_raw1")
             for t in range(PACK):
                 nc.scalar.activation(sine[:, t, :], h1[t][:, c0:c1], SIN)
             for t in range(PACK):
@@ -255,6 +256,12 @@ def tile_list_wagon_train_scores_kernel(
         rows_a = z2_rows(a0, a1)
         w4_q = [quantize_weight_half(w4_raw, 0, "w4_0", "w1_1_codes")]
         z2_a = quantize_rows(rows_a, "z2_a")
+        wx_plane = zeroed_plane(nc.vector, 2 * N, "wx_plane", "z2_a_bf")
+        for q in range(4):
+            nc.sync.dma_start(
+                wx_plane[32 * q : 32 * q + 4, :].bitcast(I32).rearrange("r (a c) -> r a c", a=2),
+                wx_scales[:, 4 * q : 4 * q + 4, :].bitcast(I32).rearrange("a r c -> r a c"),
+            )
         rows_b = z2_rows(b0, b1)
         wx_codes = held([P, 2, 2 * N], U8, "wx_codes", picked_slots[0])
         nc.sync.dma_start(wx_codes[:].bitcast(I32), wx_words.bitcast(I32).rearrange("a p c -> p a c"))

@@ -21,6 +21,9 @@ COPY = mybir.ActivationFunctionType.Copy
 P = 128
 PACK = 4
 BANK = 512
+H2_BANKS = (2, 4, 6, 7)
+SPARE_BANKS = (0, 1, 3, 5)
+WAGON_BANKS = (H2_BANKS[:2], H2_BANKS[2:], SPARE_BANKS)
 TRAIN_CHUNKS = ((0, 256), (256, 512))
 WAGON_CHUNKS = ((0, 256), (256, 512), (512, 1024))
 
@@ -39,7 +42,7 @@ def tile_list_wagon_train_scores_kernel(
     nc = tc.nc
     with ExitStack() as ctx:
         keep = ctx.enter_context(tc.tile_pool(name="keep", bufs=1))
-        psum = ctx.enter_context(tc.psum_pool(name="psum", bufs=8))
+        psum = ctx.enter_context(tc.psum_pool(name="psum", bufs=1))
 
         def held(shape, dtype, name, slot=None):
             return keep.tile(shape, dtype, name=name, tag=slot or name, align_bytes=64)
@@ -72,9 +75,16 @@ def tile_list_wagon_train_scores_kernel(
         def block(i):
             return slice(P * i, P * (i + 1))
 
+        def bank(b):
+            return psum.tile([P, BANK], F32, name="acc", tag="bank%d" % b)
+
         def load_scales(queue, plane, src):
             for q in range(4):
                 queue.dma_start(plane[32 * q : 32 * q + 4, :].bitcast(I32), src[4 * q : 4 * q + 4, :].bitcast(I32))
+
+        warm = held([P, 16], F32, "warm")
+        nc.gpsimd.memset(warm[:, 0:1], 0.0)
+        nc.scalar.activation(warm[:, 8:9], warm[:, 0:1], SIN)
 
         tab_plane = zeroed_plane(nc.vector, T, "tab_plane")
         tab2_plane = zeroed_plane(nc.gpsimd, T, "tab2_plane")
@@ -146,7 +156,6 @@ def tile_list_wagon_train_scores_kernel(
         w4_raw = load_rows(w4, "w4_raw", "w2_raw1")
         w1_q0 = quantize(w1_bf0[:], "w1_0")
         v2_plane = gather(tab2_plane[:], idx2, P2, U8, "v2_plane", "w1_bf0")
-        wg2_sb = load_plain(wg2, "wg2_sb", "tab2_plane")
         w1_bf1 = held([P, PACK * H], BF16, "w1_bf1")
         for u in range(2):
             deal_w1(w1_bf1, w1_raw1[u], 64 * u)
@@ -168,11 +177,11 @@ def tile_list_wagon_train_scores_kernel(
         for t in range(PACK):
             for u in range(2):
                 cols = slice(BANK * u, BANK * (u + 1))
-                h1_acc[t, u] = psum.tile([P, BANK], F32, name="acc")
+                h1_acc[t, u] = bank(2 * t + u)
                 mx(h1_acc[t, u][:], w1_q0[0][:, block(t)].bitcast(FP8X4), w1_q0[1][:, block(t)],
                    v0[:, cols].bitcast(FP8X4), v_plane[:, cols], True, False)
         pages[0] = load_plain(page1[block(0), :], "page0", "w1_0_codes")
-        w3_raw = load_rows(w3, "w3_raw", "w1_0_plane")
+        wg2_sb = load_plain(wg2, "wg2_sb", "w1_0_plane")
         h1 = []
         h2_acc = []
         for t in range(PACK):
@@ -182,10 +191,12 @@ def tile_list_wagon_train_scores_kernel(
                 mx(h1_acc[t, u][:], w1_q1[0][:, block(t)].bitcast(FP8X4), w1_q1[1][:, block(t)],
                    v1[:, cols].bitcast(FP8X4), v_plane[4:P, cols], False, True)
                 nc.scalar.copy(h1[t][:, cols], h1_acc[t, u][:])
-            h2_acc.append(psum.tile([P, BANK], F32, name="acc"))
+        for t in range(PACK):
+            h2_acc.append(bank(H2_BANKS[t]))
             mx(h2_acc[t][:], w2_codes[:, 2 * P * t : 2 * P * (t + 1)].bitcast(FP4X4), w2_plane[:, block(t)],
                v2[:].bitcast(FP8X4), v2_plane[:], True, True)
 
+        w3_raw = load_rows(w3, "w3_raw", "w1_bf1")
         pages[2] = load_plain(page1[block(2), :], "page2", "w1_bf0")
         pages[3] = load_plain(page1[block(3), :], "page3", "w2_plane_raw")
         picked_slots = ("tab0", "picked1", "picked2", "picked3")
@@ -195,47 +206,52 @@ def tile_list_wagon_train_scores_kernel(
             interleave(nc, bf[:], raw[:, :, 256 * u : 256 * (u + 1)])
             return quantize(bf[:], name)
 
-        def z2_rows(c0, c1):
-            rows = held([P, PACK, c1 - c0], BF16, "z2_rows%d" % c0)
-            for t in range(PACK):
-                picked = held([P, c1 - c0], F32, "picked%d_%d" % (c0, t), picked_slots[t])
-                nc.vector.tensor_copy(picked[:], h1[t][:].indirect(pilot[:, c0 // 16 : c1 // 16]))
-                nc.vector.scalar_tensor_tensor(
-                    rows[:, t, :], picked[:], pv_col[:, t : t + 1], h2_acc[t][:, c0:c1], MULT, MAX
-                )
-            return rows
+        def pick_pilots(picked, t, c0, c1):
+            nc.vector.tensor_copy(picked, h1[t][:].indirect(pilot[:, c0 // 16 : c1 // 16]))
 
-        def z1_rows(c0, c1):
-            rows = held([P, PACK, c1 - c0], BF16, "z1_rows%d" % c0)
+        def z2_row(rows, picked, t, c0, c1):
+            nc.vector.scalar_tensor_tensor(
+                rows[:, t, :], picked, pv_col[:, t : t + 1], h2_acc[t][:, c0:c1], MULT, MAX
+            )
+
+        def sines(c0, c1):
             sine = held([P, PACK, c1 - c0], F32, "sine%d" % c0, "w2_raw1")
             for t in range(PACK):
                 nc.scalar.activation(sine[:, t, :], h1[t][:, c0:c1], SIN)
+            return sine
+
+        def z1_rows(sine, name):
+            rows = held(list(sine.shape), BF16, name)
             for t in range(PACK):
                 nc.scalar.activation(rows[:, t, :], sine[:, t, :], COPY, scale=gz_col[:, t : t + 1])
             return rows
 
-        def quantize_rows(rows, name, slot=None):
-            bf = held([P, PACK * rows.shape[2]], BF16, name + "_bf")
+        def quantize_rows(rows, name, slot=None, bf_slot=None):
+            bf = held([P, PACK * rows.shape[2]], BF16, name + "_bf", bf_slot)
             interleave(nc, bf[:], rows[:])
             return quantize(bf[:], name, slot)
 
         def scatter(n, lst, c0, c1, y, gains):
             nc.vector.tensor_tensor(pages[n][:].indirect(lst[:, c0 // 16 : c1 // 16]), y, gains[:, c0:c1], MULT)
 
-        def train_scores(u, z2_q, w4_q, c0, c1):
+        def train_scores(b, u, z2_q, w4_q, c0, c1, slots):
             width = c1 - c0
-            acc = psum.tile([P, BANK], F32, name="acc")
+            acc = bank(b)
             for e in range(2):
                 mx(acc[:, width * e : width * (e + 1)], w4_q[0][:, block(e)].bitcast(FP8X4), w4_q[1][:, block(e)],
                    z2_q[0][:].bitcast(FP8X4), z2_q[1][:], True, True)
-            y = held([P, BANK], F32, "y2_%d_%d" % (c0, u))
-            nc.scalar.copy(y[:], acc[:])
+            span = BANK // len(slots)
+            ys = []
+            for e, slot in enumerate(slots):
+                ys.append(held([P, span], F32, "y2_%d_%d_%d" % (c0, u, e), slot))
+                nc.scalar.copy(ys[e][:], acc[:, span * e : span * (e + 1)])
             for e in range(2):
-                scatter(2 * u + e, slots2, c0, c1, y[:, width * e : width * (e + 1)], wg2_sb)
+                y, first = ys[width * e // span], width * e % span
+                scatter(2 * u + e, slots2, c0, c1, y[:, first : first + width], wg2_sb)
 
-        def wagon_scores(ns, z1_q, w3_q, c0, c1):
+        def wagon_scores(b, ns, z1_q, w3_q, c0, c1):
             width = c1 - c0
-            acc = psum.tile([P, BANK], F32, name="acc")
+            acc = bank(b)
             for e, n in enumerate(ns):
                 dst = acc[:, width * e : width * (e + 1)]
                 for a, (words, plane) in enumerate(((v0, v_plane), (v1, v1_plane))):
@@ -253,33 +269,45 @@ def tile_list_wagon_train_scores_kernel(
                     nc.sync.dma_start(out[block(n), :], pages[n][:])
 
         (a0, a1), (b0, b1) = TRAIN_CHUNKS
-        rows_a = z2_rows(a0, a1)
+        rows_a = held([P, PACK, a1 - a0], BF16, "z2_rows0")
+        for t in range(PACK):
+            picked = held([P, a1 - a0], F32, "picked_a%d" % t, picked_slots[t])
+            pick_pilots(picked[:], t, a0, a1)
+            z2_row(rows_a, picked[:], t, a0, a1)
         w4_q = [quantize_weight_half(w4_raw, 0, "w4_0", "w1_1_codes")]
         z2_a = quantize_rows(rows_a, "z2_a")
-        wx_plane = zeroed_plane(nc.vector, 2 * N, "wx_plane", "z2_a_bf")
+        rows_b = held([P, PACK, b1 - b0], BF16, "z2_rows256")
+        picked_b = held([P, PACK - 1, b1 - b0], F32, "picked_b", picked_slots[3])
+        for t in range(PACK - 1):
+            pick_pilots(picked_b[:, t, :], t, b0, b1)
+        for t in range(PACK - 1):
+            z2_row(rows_b, picked_b[:, t, :], t, b0, b1)
+        picked_last = held([P, b1 - b0], F32, "picked_last", "z2_a_bf")
+        pick_pilots(picked_last[:], PACK - 1, b0, b1)
+        z2_row(rows_b, picked_last[:], PACK - 1, b0, b1)
+        wx_plane = zeroed_plane(nc.vector, 2 * N, "wx_plane", "z2_rows0")
         for q in range(4):
             nc.sync.dma_start(
                 wx_plane[32 * q : 32 * q + 4, :].bitcast(I32).rearrange("r (a c) -> r a c", a=2),
                 wx_scales[:, 4 * q : 4 * q + 4, :].bitcast(I32).rearrange("a r c -> r a c"),
             )
-        rows_b = z2_rows(b0, b1)
-        wx_codes = held([P, 2, 2 * N], U8, "wx_codes", picked_slots[0])
+        wx_codes = held([P, 2, 2 * N], U8, "wx_codes", picked_slots[3])
         nc.sync.dma_start(wx_codes[:].bitcast(I32), wx_words.bitcast(I32).rearrange("a p c -> p a c"))
-        wg1_sb = load_plain(wg1, "wg1_sb", picked_slots[1])
-        train_scores(0, z2_a, w4_q[0], a0, a1)
+        wg1_sb = load_plain(wg1, "wg1_sb", "z2_a_bf")
+        train_scores(SPARE_BANKS[0], 0, z2_a, w4_q[0], a0, a1, ("y_first", "y_second"))
         w4_q.append(quantize_weight_half(w4_raw, 1, "w4_1", "w1_1_plane"))
-        train_scores(1, z2_a, w4_q[1], a0, a1)
-        z2_b = quantize_rows(rows_b, "z2_b")
-        train_scores(0, z2_b, w4_q[0], b0, b1)
-        z1_q = quantize_rows(z1_rows(*WAGON_CHUNKS[0]), "z1_0", "y2_0_1")
-        w3_q = [quantize_weight_half(w3_raw, u, "w3_%d" % u, slot) for u, slot in enumerate(("z2_rows256", "z2_b_bf"))]
-        train_scores(1, z2_b, w4_q[1], b0, b1)
-        for i, (c0, c1) in enumerate(WAGON_CHUNKS):
-            per_bank = BANK // (c1 - c0)
-            groups = [range(n0, n0 + per_bank) for n0 in range(0, 4, per_bank)]
-            for ns in groups[:-1]:
-                wagon_scores(ns, z1_q, w3_q, c0, c1)
-            if i + 1 < len(WAGON_CHUNKS):
-                z1_next = quantize_rows(z1_rows(*WAGON_CHUNKS[i + 1]), "z1_%d" % (i + 1), "y1_%d_0" % c0)
-            wagon_scores(groups[-1], z1_q, w3_q, c0, c1)
-            z1_q = z1_next
+        first_sines = sines(*WAGON_CHUNKS[0])
+        z2_b = quantize_rows(rows_b, "z2_b", bf_slot="y_first")
+        train_scores(SPARE_BANKS[1], 1, z2_a, w4_q[1], a0, a1, ("z2_rows256",))
+        train_scores(SPARE_BANKS[2], 0, z2_b, w4_q[0], b0, b1, ("y2_256_0",))
+        w3_q = [quantize_weight_half(w3_raw, 0, "w3_0", "y_first")]
+        z1_q = [quantize_rows(z1_rows(first_sines, "z1_rows0"), "z1_0", "z2_rows256")]
+        train_scores(SPARE_BANKS[3], 1, z2_b, w4_q[1], b0, b1, ("y2_256_1",))
+        w3_q.append(quantize_weight_half(w3_raw, 1, "w3_1", "z1_rows0"))
+        for i, (c0, c1) in enumerate(WAGON_CHUNKS[:-1]):
+            rows = z1_rows(sines(*WAGON_CHUNKS[i + 1]), "z1_rows%d" % (i + 1))
+            wagon_scores(WAGON_BANKS[i][0], (0, 1), z1_q[i], w3_q, c0, c1)
+            z1_q.append(quantize_rows(rows, "z1_%d" % (i + 1), ("y2_256_1", "y1_0_2")[i]))
+            wagon_scores(WAGON_BANKS[i][1], (2, 3), z1_q[i], w3_q, c0, c1)
+        for n in range(4):
+            wagon_scores(WAGON_BANKS[-1][n], (n,), z1_q[-1], w3_q, *WAGON_CHUNKS[-1])

from contextlib import ExitStack

import concourse.mybir as mybir

K, K2, H, N, T, S, P2, T2 = 1024, 512, 512, 512, 2048, 1024, 512, 2048
FLOPS = 2 * (K * H * S + K2 * H * P2 + H * N * S + K * N * S + H * N * P2)

F32 = mybir.dt.float32
BF16 = mybir.dt.bfloat16
I32 = mybir.dt.int32
U32 = mybir.dt.uint32
U16 = mybir.dt.uint16
U8 = mybir.dt.uint8
FP8X4 = mybir.dt.float8_e4m3fn_x4
FP4X4 = mybir.dt.float4_e2m1fn_x4
MULT = mybir.AluOpType.mult
MAX = mybir.AluOpType.max
SIN = mybir.ActivationFunctionType.Sin
COPY = mybir.ActivationFunctionType.Copy

P = 128
PACK = 4
BANK = 512
H2_BANKS = (2, 4, 6, 7)
SPARE_BANKS = (0, 1, 3, 5)
WAGON_BANKS = (H2_BANKS[:2], H2_BANKS[2:], SPARE_BANKS)
TRAIN_CHUNKS = ((0, 256), (256, 512))
WAGON_CHUNKS = ((0, 256), (256, 512), (512, 1024))


def interleave(nc, dst, src):
    nc.scalar.copy(
        dst.rearrange("p (c i t) -> p c t i", i=4, t=PACK),
        src.rearrange("p t (c i) -> p c t i", i=4),
    )


def tile_list_wagon_train_scores_kernel(
    tc, tab_words, tab_scales, tab2_words, tab2_scales, offs, offs2, pos1, offs3, offs4,
    w1, w2_words, w2_scales, w3, wx_words, wx_scales, w4, gz, pv, wg1, wg2, page1, out,
):
    nc = tc.nc
    with ExitStack() as ctx:
        keep = ctx.enter_context(tc.tile_pool(name="keep", bufs=1))
        psum = ctx.enter_context(tc.psum_pool(name="psum", bufs=1))

        def held(shape, dtype, name, slot=None):
            return keep.tile(shape, dtype, name=name, tag=slot or name, align_bytes=64)

        def load_list(src, name):
            lst = held(list(src.shape), U16, name)
            nc.sync.dma_start(lst[:], src)
            return lst

        def load_words(src, name, slot=None):
            words = held([P, T], I32, name, slot)
            nc.sync.dma_start(words[:], src.rearrange("p t i -> p (t i)").bitcast(I32))
            return words

        def load_rows(src, name, slot=None):
            rows = held([P, PACK, src.shape[1]], F32, name, slot)
            nc.sync.dma_start(rows[:], src.rearrange("(p j) c -> p j c", j=PACK))
            return rows

        def zeroed_plane(engine, width, name, slot=None):
            plane = held([P, width], U8, name, slot)
            engine.memset(plane[:].bitcast(I32), 0)
            return plane

        def load_plain(src, name, slot):
            rows = held(list(src.shape), F32, name, slot)
            nc.sync.dma_start(rows[:], src)
            return rows

        def block(i):
            return slice(P * i, P * (i + 1))

        def bank(b):
            return psum.tile([P, BANK], F32, name="acc", tag="bank%d" % b)

        def load_scales(queue, plane, src):
            for q in range(4):
                queue.dma_start(plane[32 * q : 32 * q + 4, :].bitcast(I32), src[4 * q : 4 * q + 4, :].bitcast(I32))

        warm = held([P, 16], F32, "warm")
        nc.gpsimd.memset(warm[:, 0:1], 0.0)
        nc.scalar.activation(warm[:, 8:9], warm[:, 0:1], SIN)

        tab_plane = zeroed_plane(nc.vector, T, "tab_plane")
        tab2_plane = zeroed_plane(nc.gpsimd, T, "tab2_plane")
        w2_plane_raw = zeroed_plane(nc.vector, H, "w2_plane_raw")
        v1_plane = zeroed_plane(nc.vector, S, "v1_plane")
        load_scales(nc.gpsimd, tab2_plane, tab2_scales[0])
        load_scales(nc.gpsimd, w2_plane_raw, w2_scales[0])

        idx = load_list(offs, "idx")
        idx2 = load_list(offs2, "idx2")
        pilot = load_list(pos1, "pilot")
        slots2 = load_list(offs4, "slots2")
        slots1 = load_list(offs3, "slots1")
        w2_raw = []
        for u in range(2):
            w2_raw.append(held([P, H // 2], U16, "w2_raw%d" % u))
            nc.sync.dma_start(w2_raw[u][:].bitcast(I32), w2_words[0, :, 512 * u : 512 * (u + 1)].bitcast(I32))
        tab0 = load_words(tab_words[0], "tab0")
        for q in range(4):
            nc.sync.dma_start(
                tab_plane[32 * q : 32 * q + 8, :].bitcast(I32), tab_scales[:, 4 * q : 4 * q + 4, :].bitcast(I32)
            )
        w2_codes = held([P, 2 * H], U8, "w2_codes")
        for u in range(2):
            nc.vector.tensor_copy(
                w2_codes[:].bitcast(U16).rearrange("p (t m) -> p t m", t=PACK)[:, :, 64 * u : 64 * (u + 1)],
                w2_raw[u][:].rearrange("p (m t) -> p t m", t=PACK),
            )
        w1_all = held([P, 2 * PACK * H], F32, "w1_all", "w2_raw0")
        w1_raw0 = w1_all[:, 0:2048].rearrange("p (j c) -> p j c", j=PACK)
        w1_raw1 = [w1_all[:, 2048 + 1024 * u : 3072 + 1024 * u].rearrange("p (j c) -> p j c", j=PACK) for u in range(2)]
        nc.sync.dma_start(w1_raw0, w1[0:512, :].rearrange("(p j) c -> p j c", j=PACK))
        tab1 = load_words(tab_words[1], "tab1", "w2_raw1")
        for u in range(2):
            nc.sync.dma_start(w1_raw1[u], w1[512:1024, 256 * u : 256 * (u + 1)].rearrange("(p j) c -> p j c", j=PACK))

        def gather(window, lst, count, dtype, name, slot=None):
            picked = held([P, count], dtype, name, slot)
            nc.vector.tensor_copy(picked[:], window.indirect(lst[:]))
            return picked

        def quantize(src, name, slot=None):
            width = src.shape[1] // PACK
            codes = held([P, width], U32, name + "_codes", slot)
            plane = held([P, width], U8, name + "_plane")
            nc.vector.quantize_mx(out=codes[:].bitcast(FP8X4), scales=plane[:], in_=src)
            return codes, plane

        def deal_w1(dst, raw, m0):
            count = raw.shape[2] // PACK
            nc.scalar.copy(
                dst[:].rearrange("p (t m j) -> p m t j", t=PACK, j=PACK)[:, m0 : m0 + count, :, :],
                raw.rearrange("p j (m t) -> p m t j", t=PACK),
            )

        pages = {}
        v0 = gather(tab0[:].bitcast(U32), idx, S, U32, "v0")
        tab2 = load_words(tab2_words[0], "tab2", "tab0")
        v_plane = gather(tab_plane[:], idx, S, U8, "v_plane")
        gains = held([P, 2, 8], F32, "gains", "tab_plane")
        pv_col = gains[:, 0, :]
        gz_col = gains[:, 1, :]
        nc.sync.dma_start(pv_col[:, 0:PACK], pv.rearrange("(p t) -> p t", t=PACK))
        nc.sync.dma_start(gz_col[:, 0:PACK], gz.rearrange("(p t) -> p t", t=PACK))
        nc.sync.dma_start(v1_plane[0:100, :].bitcast(I32), v_plane[4:104, :].bitcast(I32))
        w1_bf0 = held([P, PACK * H], BF16, "w1_bf0")
        deal_w1(w1_bf0, w1_raw0, 0)
        v1 = gather(tab1[:].bitcast(U32), idx, S, U32, "v1")
        w4_raw = load_rows(w4, "w4_raw", "w2_raw1")
        w1_q0 = quantize(w1_bf0[:], "w1_0")
        v2_plane = gather(tab2_plane[:], idx2, P2, U8, "v2_plane", "w1_bf0")
        w1_bf1 = held([P, PACK * H], BF16, "w1_bf1")
        for u in range(2):
            deal_w1(w1_bf1, w1_raw1[u], 64 * u)
        pages[1] = load_plain(page1[block(1), :], "page1", "w2_raw0")
        w1_q1 = quantize(w1_bf1[:], "w1_1")
        w2_plane = held([P, H], U8, "w2_plane", "w1_bf1")
        nc.vector.tensor_copy(
            w2_plane[:].rearrange("p (t m) -> p t m", t=PACK),
            w2_plane_raw[:].rearrange("p (m t) -> p t m", t=PACK),
        )
        v2 = gather(tab2[:].bitcast(U32), idx2, P2, U32, "v2", "w2_plane_raw")

        def mx(acc, lhs, lhs_plane, rhs, rhs_plane, start, stop):
            nc.tensor.matmul_mx(
                out=acc, lhsT=lhs, lhsT_scale=lhs_plane, rhs=rhs, rhs_scale=rhs_plane, start=start, stop=stop
            )

        h1_acc = {}
        for t in range(PACK):
            for u in range(2):
                cols = slice(BANK * u, BANK * (u + 1))
                h1_acc[t, u] = bank(2 * t + u)
                mx(h1_acc[t, u][:], w1_q0[0][:, block(t)].bitcast(FP8X4), w1_q0[1][:, block(t)],
                   v0[:, cols].bitcast(FP8X4), v_plane[:, cols], True, False)
        pages[0] = load_plain(page1[block(0), :], "page0", "w1_0_codes")
        wg2_sb = load_plain(wg2, "wg2_sb", "w1_0_plane")
        h1 = []
        h2_acc = []
        for t in range(PACK):
            h1.append(held([P, S], F32, "h1_%d" % t))
            for u in range(2):
                cols = slice(BANK * u, BANK * (u + 1))
                mx(h1_acc[t, u][:], w1_q1[0][:, block(t)].bitcast(FP8X4), w1_q1[1][:, block(t)],
                   v1[:, cols].bitcast(FP8X4), v_plane[4:P, cols], False, True)
                nc.scalar.copy(h1[t][:, cols], h1_acc[t, u][:])
        for t in range(PACK):
            h2_acc.append(bank(H2_BANKS[t]))
            mx(h2_acc[t][:], w2_codes[:, 2 * P * t : 2 * P * (t + 1)].bitcast(FP4X4), w2_plane[:, block(t)],
               v2[:].bitcast(FP8X4), v2_plane[:], True, True)

        w3_raw = load_rows(w3, "w3_raw", "w1_bf1")
        pages[2] = load_plain(page1[block(2), :], "page2", "w1_bf0")
        pages[3] = load_plain(page1[block(3), :], "page3", "w2_plane_raw")
        picked_slots = ("tab0", "picked1", "picked2", "picked3")

        def quantize_weight_half(raw, u, name, slot):
            bf = held([P, PACK * 256], BF16, name + "_bf", slot)
            interleave(nc, bf[:], raw[:, :, 256 * u : 256 * (u + 1)])
            return quantize(bf[:], name)

        def pick_pilots(picked, t, c0, c1):
            nc.vector.tensor_copy(picked, h1[t][:].indirect(pilot[:, c0 // 16 : c1 // 16]))

        def z2_row(rows, picked, t, c0, c1):
            nc.vector.scalar_tensor_tensor(
                rows[:, t, :], picked, pv_col[:, t : t + 1], h2_acc[t][:, c0:c1], MULT, MAX
            )

        def sines(c0, c1):
            sine = held([P, PACK, c1 - c0], F32, "sine%d" % c0, "w2_raw1")
            for t in range(PACK):
                nc.scalar.activation(sine[:, t, :], h1[t][:, c0:c1], SIN)
            return sine

        def z1_rows(sine, name):
            rows = held(list(sine.shape), BF16, name)
            for t in range(PACK):
                nc.scalar.activation(rows[:, t, :], sine[:, t, :], COPY, scale=gz_col[:, t : t + 1])
            return rows

        def quantize_rows(rows, name, slot=None, bf_slot=None):
            bf = held([P, PACK * rows.shape[2]], BF16, name + "_bf", bf_slot)
            interleave(nc, bf[:], rows[:])
            return quantize(bf[:], name, slot)

        def scatter(n, lst, c0, c1, y, gains):
            nc.vector.tensor_tensor(pages[n][:].indirect(lst[:, c0 // 16 : c1 // 16]), y, gains[:, c0:c1], MULT)

        def train_scores(b, u, z2_q, w4_q, c0, c1, slots):
            width = c1 - c0
            acc = bank(b)
            for e in range(2):
                mx(acc[:, width * e : width * (e + 1)], w4_q[0][:, block(e)].bitcast(FP8X4), w4_q[1][:, block(e)],
                   z2_q[0][:].bitcast(FP8X4), z2_q[1][:], True, True)
            span = BANK // len(slots)
            ys = []
            for e, slot in enumerate(slots):
                ys.append(held([P, span], F32, "y2_%d_%d_%d" % (c0, u, e), slot))
                nc.scalar.copy(ys[e][:], acc[:, span * e : span * (e + 1)])
            for e in range(2):
                y, first = ys[width * e // span], width * e % span
                scatter(2 * u + e, slots2, c0, c1, y[:, first : first + width], wg2_sb)

        def wagon_scores(b, ns, z1_q, w3_q, c0, c1):
            width = c1 - c0
            acc = bank(b)
            for e, n in enumerate(ns):
                dst = acc[:, width * e : width * (e + 1)]
                for a, (words, plane) in enumerate(((v0, v_plane), (v1, v1_plane))):
                    mx(dst, wx_codes[:, a, 2 * P * n : 2 * P * (n + 1)].bitcast(FP4X4),
                       wx_plane[:, N * a + P * n : N * a + P * (n + 1)],
                       words[:, c0:c1].bitcast(FP8X4), plane[:, c0:c1], a == 0, False)
                w3_codes, w3_plane = w3_q[n // 2]
                mx(dst, w3_codes[:, block(n % 2)].bitcast(FP8X4), w3_plane[:, block(n % 2)],
                   z1_q[0][:].bitcast(FP8X4), z1_q[1][:], False, True)
            y = held([P, BANK], F32, "y1_%d_%d" % (c0, ns[0]))
            nc.scalar.copy(y[:], acc[:])
            for e, n in enumerate(ns):
                scatter(n, slots1, c0, c1, y[:, width * e : width * (e + 1)], wg1_sb)
                if c1 == S:
                    nc.sync.dma_start(out[block(n), :], pages[n][:])

        (a0, a1), (b0, b1) = TRAIN_CHUNKS
        rows_a = held([P, PACK, a1 - a0], BF16, "z2_rows0")
        for t in range(PACK):
            picked = held([P, a1 - a0], F32, "picked_a%d" % t, picked_slots[t])
            pick_pilots(picked[:], t, a0, a1)
            z2_row(rows_a, picked[:], t, a0, a1)
        w4_q = [quantize_weight_half(w4_raw, 0, "w4_0", "w1_1_codes")]
        z2_a = quantize_rows(rows_a, "z2_a")
        rows_b = held([P, PACK, b1 - b0], BF16, "z2_rows256")
        picked_b = held([P, PACK - 1, b1 - b0], F32, "picked_b", picked_slots[3])
        for t in range(PACK - 1):
            pick_pilots(picked_b[:, t, :], t, b0, b1)
        for t in range(PACK - 1):
            z2_row(rows_b, picked_b[:, t, :], t, b0, b1)
        picked_last = held([P, b1 - b0], F32, "picked_last", "z2_a_bf")
        pick_pilots(picked_last[:], PACK - 1, b0, b1)
        z2_row(rows_b, picked_last[:], PACK - 1, b0, b1)
        wx_plane = zeroed_plane(nc.vector, 2 * N, "wx_plane", "z2_rows0")
        for q in range(4):
            nc.sync.dma_start(
                wx_plane[32 * q : 32 * q + 4, :].bitcast(I32).rearrange("r (a c) -> r a c", a=2),
                wx_scales[:, 4 * q : 4 * q + 4, :].bitcast(I32).rearrange("a r c -> r a c"),
            )
        wx_codes = held([P, 2, 2 * N], U8, "wx_codes", picked_slots[3])
        nc.sync.dma_start(wx_codes[:].bitcast(I32), wx_words.bitcast(I32).rearrange("a p c -> p a c"))
        wg1_sb = load_plain(wg1, "wg1_sb", "z2_a_bf")
        train_scores(SPARE_BANKS[0], 0, z2_a, w4_q[0], a0, a1, ("y_first", "y_second"))
        w4_q.append(quantize_weight_half(w4_raw, 1, "w4_1", "w1_1_plane"))
        first_sines = sines(*WAGON_CHUNKS[0])
        z2_b = quantize_rows(rows_b, "z2_b", bf_slot="y_first")
        train_scores(SPARE_BANKS[1], 1, z2_a, w4_q[1], a0, a1, ("z2_rows256",))
        train_scores(SPARE_BANKS[2], 0, z2_b, w4_q[0], b0, b1, ("y2_256_0",))
        w3_q = [quantize_weight_half(w3_raw, 0, "w3_0", "y_first")]
        z1_q = [quantize_rows(z1_rows(first_sines, "z1_rows0"), "z1_0", "z2_rows256")]
        train_scores(SPARE_BANKS[3], 1, z2_b, w4_q[1], b0, b1, ("y2_256_1",))
        w3_q.append(quantize_weight_half(w3_raw, 1, "w3_1", "z1_rows0"))
        for i, (c0, c1) in enumerate(WAGON_CHUNKS[:-1]):
            rows = z1_rows(sines(*WAGON_CHUNKS[i + 1]), "z1_rows%d" % (i + 1))
            wagon_scores(WAGON_BANKS[i][0], (0, 1), z1_q[i], w3_q, c0, c1)
            z1_q.append(quantize_rows(rows, "z1_%d" % (i + 1), ("y2_256_1", "y1_0_2")[i]))
            wagon_scores(WAGON_BANKS[i][1], (2, 3), z1_q[i], w3_q, c0, c1)
        for n in range(4):
            wagon_scores(WAGON_BANKS[-1][n], (n,), z1_q[-1], w3_q, *WAGON_CHUNKS[-1])
